import numpy as np
import ml_dtypes


def mxq(x, axis, fmt="e4m3"):
    dtype, down = {"e4m3": (ml_dtypes.float8_e4m3fn, 7), "e5m2": (ml_dtypes.float8_e5m2, 14)}[fmt]
    v = np.moveaxis(np.asarray(x, np.float32).astype(ml_dtypes.bfloat16).astype(np.float64), axis, -1)
    blocks = v.reshape(v.shape[:-1] + (-1, 32))
    amax = np.abs(blocks).max(-1, keepdims=True)
    byte = np.maximum(np.where(amax > 0, np.frexp(amax)[1] - 1 + 127, 0) - down, 1)
    scale = np.exp2(byte - 127.0)
    codes = (blocks / scale).astype(np.float32).astype(dtype).astype(np.float64)
    return np.moveaxis((codes * scale).reshape(v.shape), -1, axis)


WIDE = False


def mx_kscale(k):
    if not WIDE:
        return np.ones(k)
    levels = np.array([10, -10, 5, -5, 0])
    if k % 512:
        return np.exp2(np.random.permutation(np.resize(levels, k // 32))).repeat(32)
    a = np.empty((k // 512, 16))
    for p in range(k // 512):
        a[p, :8] = np.random.permutation(np.resize(levels, 8))
        for g in range(8):
            far = levels[np.abs(levels - a[p, g]) >= 10]
            a[p, g + 8] = far[np.random.randint(len(far))]
    return np.exp2(a.ravel()).repeat(32)


def f64(x):
    return np.asarray(x).astype(np.float64)


def striped(idx):
    return np.tile(idx.reshape(-1, 16).T, (8, 1)).astype(np.uint16)


def unstriped(offs):
    return offs[:16].T.reshape(-1).astype(np.int64)


E2M1 = np.array([0.0, 0.5, 1.0, 1.5, 2.0, 3.0, 4.0, 6.0, -0.0, -0.5, -1.0, -1.5, -2.0, -3.0, -4.0, -6.0])


def pack_weight(w, fmt):
    k, n = w.shape
    w = f64(np.asarray(w, np.float32).astype(ml_dtypes.bfloat16)).reshape(k // 32, 32, n)
    amax = np.abs(w).max(1)
    if fmt == "e4m3":
        byte = np.frexp(amax)[1] - 1 + 127 - 7
    else:
        mant, ex = np.frexp(amax / 6.0)
        byte = np.where(mant > 0.5, ex, ex - 1) + 127
    byte = np.clip(np.where(amax > 0, byte, 1), 1, 254)
    scaled = (w * np.exp2(127.0 - byte)[:, None, :]).reshape(k, n).astype(np.float32)
    by_word = np.ascontiguousarray(scaled.reshape(k // 512, 128, 4, n).transpose(0, 1, 3, 2))
    if fmt == "e4m3":
        words = by_word.astype(ml_dtypes.float8_e4m3fn).view(np.uint8)
    else:
        c = by_word.astype(ml_dtypes.float4_e2m1fn).view(np.uint8) & 0xF
        words = (c[..., 0::2] | (c[..., 1::2] << 4)).reshape(k // 512, 128, 2 * n)
    return np.ascontiguousarray(words), np.ascontiguousarray(byte.astype(np.uint8).reshape(k // 512, 16, n))


def unpack_weight(words, scales, fmt):
    g, _, n = scales.shape
    words = np.ascontiguousarray(words).reshape(g, 128, n, -1)
    if fmt == "e4m3":
        vals = words.view(ml_dtypes.float8_e4m3fn).astype(np.float64)
    else:
        nib = np.empty((g, 128, n, 4), np.uint8)
        nib[..., 0::2] = words & 0xF
        nib[..., 1::2] = words >> 4
        vals = E2M1[nib]
    vals = vals * np.repeat(np.exp2(scales.astype(np.float64) - 127.0), 8, axis=1)[..., None]
    return vals.transpose(0, 1, 3, 2).reshape(g * 512, n)


def gelu(v):
    return 0.5 * v * (1.0 + np.tanh(np.sqrt(2.0 / np.pi) * (v + 0.044715 * v**3)))


def bf(x):
    return np.asarray(x, np.float32).astype(ml_dtypes.bfloat16)


def planes(Y):
    n, m = Y.shape
    b = f64(bf(Y)).reshape(n // 32, 32, m)
    amax = np.abs(b).max(1)
    byte = np.clip(np.where(amax > 0, np.frexp(amax)[1] - 1 + 127 - 7, 1), 1, 254)
    codes = (b * np.exp2(127.0 - byte)[:, None, :]).reshape(n, m).astype(np.float32).astype(ml_dtypes.float8_e4m3fn).view(np.uint8)
    words = codes.reshape(n // 512, 128, 4, m).transpose(0, 1, 3, 2)
    return np.ascontiguousarray(words), np.ascontiguousarray(byte.astype(np.uint8).reshape(n // 512, 16, m))


K, T, S, P, P2, H, N = 512, 4096, 1024, 512, 256, 1024, 1024

def setup_inputs():
    n = np.random.standard_normal
    s = mx_kscale(K)[:, None]
    u = mx_kscale(H)[:, None]
    tab_words, tab_scales = pack_weight(n((K, T)) * s, "e4m3")
    w1 = (1.2 * n((K, H)) / np.sqrt(K) / s).astype(np.float32)
    w2_words, w2_scales = pack_weight(1.2 * n((K, H)) / np.sqrt(K) / s, "e2m1")
    w3 = (1.2 * n((K, H)) / np.sqrt(K) / s).astype(np.float32)
    gain = (u[:, 0] * np.exp(0.3 * n(H))).astype(np.float32)
    size = np.exp(0.8 * n(N))[None, :]
    wo_words, wo_scales = pack_weight(1.5 * n((H, N)) / np.sqrt(H) / u * size, "e4m3")
    perm = np.random.permutation(S)
    return {"tab_words": tab_words, "tab_scales": tab_scales,
            "offs": striped(np.random.permutation(T)[:S]),
            "pos1": striped(perm[:P]), "pos2": striped(perm[P:2 * P]),
            "pos3": striped(np.random.permutation(P)[:P2]),
            "pos4": striped(np.random.permutation(S)[:P2]),
            "w1": w1, "w2_words": w2_words, "w2_scales": w2_scales, "w3": w3,
            "gain": gain, "wo_words": wo_words, "wo_scales": wo_scales}

def reference(tab_words, tab_scales, offs, pos1, pos2, pos3, pos4, w1, w2_words, w2_scales, w3, gain, wo_words, wo_scales):
    v = unpack_weight(tab_words, tab_scales, "e4m3")[:, unstriped(offs)]
    w2 = unpack_weight(w2_words, w2_scales, "e2m1")
    wo = unpack_weight(wo_words, wo_scales, "e4m3")
    h = mxq(f64(w1), 0, "e4m3").T @ v
    h = np.maximum(h, w2.T @ v)
    h = np.maximum(h, mxq(f64(w3), 0, "e4m3").T @ v)
    a1 = h[:, unstriped(pos1)] - h[:, unstriped(pos2)]
    a2 = a1[:, unstriped(pos3)] * np.tanh(h[:, unstriped(pos4)])
    x = f64(gain)[:, None] * a2
    y = (wo.T @ mxq(x, 0, "e4m3")) + a2
    words, scales = planes(y)
    return y, words, scales

@@ -1,0 +1,287 @@
+from contextlib import ExitStack
+
+import concourse.mybir as mybir
+
+K, T, S, PAIRS, KEPT, H, N = 512, 4096, 1024, 512, 256, 1024, 1024
+FLOPS = 2 * (3 * K * H * S + H * N * KEPT)
+
+F32 = mybir.dt.float32
+BF16 = mybir.dt.bfloat16
+I32 = mybir.dt.int32
+U32 = mybir.dt.uint32
+U16 = mybir.dt.uint16
+U8 = mybir.dt.uint8
+FP8X4 = mybir.dt.float8_e4m3fn_x4
+FP4X4 = mybir.dt.float4_e2m1fn_x4
+ALU = mybir.AluOpType
+ACT = mybir.ActivationFunctionType
+
+P = 128
+PACK = 4
+GROUP = P * PACK
+GROUPS = H // GROUP
+SLICES = GROUPS * PACK
+BANK = 512
+HALVES = 2
+KEPT_HALF = KEPT // HALVES
+QUADS = 4
+
+
+def tile_list_footage_pair_features_kernel(
+    tc, tab_words, tab_scales, offs, pos1, pos2, pos3, pos4, w1, w2_words, w2_scales, w3, gain,
+    wo_words, wo_scales, out_0, out_1, out_2,
+):
+    nc = tc.nc
+    with ExitStack() as ctx:
+        keep = ctx.enter_context(tc.tile_pool(name="keep", bufs=1))
+        ring = ctx.enter_context(tc.tile_pool(name="ring", bufs=2))
+        psum = ctx.enter_context(tc.psum_pool(name="psum", bufs=1))
+
+        def load_list(src, name):
+            lst = keep.tile(list(src.shape), U16, name=name)
+            nc.sync.dma_start(lst[:], src)
+            return lst
+
+        offs_sb = load_list(offs, "offs_sb")
+        tab_s = keep.tile([P, T], U8, name="tab_s", align_bytes=64)
+        nc.vector.memset(tab_s[:].bitcast(I32), 0)
+        w_s_raw = keep.tile([P, H], U8, name="w_s_raw", align_bytes=64)
+        nc.vector.memset(w_s_raw[:].bitcast(I32), 0)
+        for q in range(QUADS):
+            nc.sync.dma_start(tab_s[32 * q : 32 * q + 4, :].bitcast(I32), tab_scales[0, 4 * q : 4 * q + 4, :].bitcast(I32))
+        tab_w = keep.tile([P, T], I32, name="tab_w", align_bytes=64)
+        nc.sync.dma_start(tab_w[:], tab_words[0].rearrange("p t i -> p (t i)").bitcast(I32))
+        w2_raw = keep.tile([P, H], U16, name="w2_raw", align_bytes=64)
+        nc.scalar.dma_start(w2_raw[:].bitcast(I32), w2_words[0].bitcast(I32))
+
+        def load_weight(w, g, name):
+            raw = keep.tile([P, PACK, GROUP], F32, name=name, align_bytes=64)
+            nc.sync.dma_start(raw[:], w[:, g * GROUP : (g + 1) * GROUP].rearrange("(p j) c -> p j c", j=PACK))
+            return raw
+
+        w_raw = {}
+        w_raw[(0, 0)] = load_weight(w1, 0, "w1_raw0")
+        for q in range(QUADS):
+            nc.scalar.dma_start(w_s_raw[32 * q : 32 * q + 4, :].bitcast(I32), w2_scales[0, 4 * q : 4 * q + 4, :].bitcast(I32))
+            nc.gpsimd.dma_start(w_s_raw[32 * q + 4 : 32 * q + 12, :].bitcast(I32), wo_scales[:, 4 * q : 4 * q + 4, :].bitcast(I32))
+        w_raw[(1, 0)] = load_weight(w3, 0, "w3_raw0")
+        pos4_sb = load_list(pos4, "pos4_sb")
+        pos2_sb = load_list(pos2, "pos2_sb")
+        pos1_sb = load_list(pos1, "pos1_sb")
+        pos3_sb = load_list(pos3, "pos3_sb")
+        gain_sb = keep.tile([P, GROUPS, PACK], F32, name="gain_sb")
+        nc.sync.dma_start(gain_sb[:], gain.rearrange("(g p t) -> p g t", g=GROUPS, t=PACK))
+        w_raw[(0, 1)] = load_weight(w1, 1, "w1_raw1")
+        w_raw[(1, 1)] = load_weight(w3, 1, "w3_raw1")
+        wo_raw = []
+        for a in range(GROUPS):
+            raw = keep.tile([P, N], I32, name="wo_raw%d" % a, align_bytes=64)
+            nc.sync.dma_start(raw[:], wo_words[a].rearrange("p c i -> p (c i)").bitcast(I32))
+            wo_raw.append(raw)
+
+        v_s = keep.tile([P, S], U8, name="v_s", align_bytes=64)
+        nc.vector.tensor_copy(v_s[:], tab_s[:].indirect(offs_sb[:]))
+        w2_q = keep.tile([P, H], U16, name="w2_q", align_bytes=64)
+        nc.vector.tensor_copy(
+            w2_q[:].rearrange("p (g t m) -> p g t m", g=GROUPS, t=PACK),
+            w2_raw[:].rearrange("p (g m t) -> p g t m", g=GROUPS, t=PACK),
+        )
+        w_s = keep.tile([P, H], U8, name="w_s", align_bytes=64)
+        nc.vector.tensor_copy(
+            w_s[:].rearrange("p (g t m) -> p g t m", g=GROUPS, t=PACK),
+            w_s_raw[:].rearrange("p (g m t) -> p g t m", g=GROUPS, t=PACK),
+        )
+        v_w = keep.tile([P, S], U32, name="v_w", align_bytes=64)
+        for c in range(HALVES):
+            nc.vector.tensor_copy(
+                v_w[:, c * BANK : (c + 1) * BANK],
+                tab_w[:].bitcast(U32).indirect(offs_sb[:, c * BANK // 16 : (c + 1) * BANK // 16]),
+            )
+
+        w_q = [keep.tile([P, H], U32, name="w_q%d" % i, align_bytes=64) for i in range(2)]
+        w_qs = [keep.tile([P, H], U8, name="w_qs%d" % i, align_bytes=64) for i in range(2)]
+        rounded = {}
+
+        def round_weight(i, s):
+            g, t = divmod(s, PACK)
+            wb = ring.tile([P, 2, P, PACK], BF16, name="w_bf", tag="w_bf", bufs=3, align_bytes=64)
+            src = w_raw[(i, g)][:].rearrange("p j (m t) -> p m t j", t=PACK)[:, :, t : t + 2, :]
+            nc.scalar.copy(wb[:].rearrange("p t m j -> p m t j"), src)
+            rounded[(i, s)] = wb
+
+        def quantise_weight(i, s):
+            cols = slice(s * P, (s + 2) * P)
+            nc.vector.quantize_mx(
+                out=w_q[i][:, cols].bitcast(FP8X4),
+                scales=w_qs[i][:, cols],
+                in_=rounded[(i, s)][:].rearrange("p t m j -> p (t m j)"),
+            )
+
+        def product(tag, bufs, codes, scales, s, c):
+            acc = psum.tile([P, BANK], F32, name="acc", tag=tag, bufs=bufs)
+            cols = slice(s * P, (s + 1) * P)
+            frames = slice(c * BANK, (c + 1) * BANK)
+            nc.tensor.matmul_mx(
+                out=acc[:], lhsT=codes(cols), lhsT_scale=scales[:, cols],
+                rhs=v_w[:, frames].bitcast(FP8X4), rhs_scale=v_s[:, frames], start=True, stop=True,
+            )
+            return acc
+
+        h12 = {}
+        h = {}
+
+        def first_max(s, c):
+            acc2 = product("acc2", 2, lambda cols: w2_q[:, cols].bitcast(FP4X4), w_s, s, c)
+            acc1 = product("acc1", 3, lambda cols: w_q[0][:, cols].bitcast(FP8X4), w_qs[0], s, c)
+            sum2 = ring.tile([P, BANK], F32, name="sum2", tag="sum2", bufs=4)
+            nc.scalar.copy(sum2[:], acc2[:])
+            h12[(s, c)] = ring.tile([P, BANK], F32, name="h12", tag="h12", bufs=6)
+            nc.vector.tensor_tensor(h12[(s, c)][:], acc1[:], sum2[:], ALU.max)
+
+        def second_max(s, c):
+            acc3 = product("acc3", 3, lambda cols: w_q[1][:, cols].bitcast(FP8X4), w_qs[1], s, c)
+            if c == 0:
+                h[s] = ring.tile([P, S], F32, name="h", tag="h", bufs=2, align_bytes=64)
+            nc.vector.tensor_tensor(h[s][:, c * BANK : (c + 1) * BANK], acc3[:], h12[(s, c)][:], ALU.max)
+
+        a2 = [keep.tile([P, PACK, KEPT], F32, name="a2_%d" % g, align_bytes=64) for g in range(GROUPS)]
+        x_bf = [keep.tile([P, KEPT, PACK], BF16, name="x_bf%d" % g, align_bytes=64) for g in range(GROUPS)]
+        x_q = [keep.tile([P, KEPT], U32, name="x_q%d" % g, align_bytes=64) for g in range(GROUPS)]
+        x_s = [keep.tile([P, KEPT], U8, name="x_s%d" % g, align_bytes=64) for g in range(GROUPS)]
+        view = {}
+        second = {}
+        a1 = {}
+
+        def pick_view(s, j0, j1):
+            picked = ring.tile([P, j1 - j0], F32, name="picked4", tag="picked4")
+            nc.vector.tensor_copy(picked[:], h[s][:].indirect(pos4_sb[:, j0 // 16 : j1 // 16]))
+            view[(s, j0)] = ring.tile([P, j1 - j0], F32, name="view", tag="view")
+            nc.scalar.activation(view[(s, j0)][:], picked[:], ACT.Tanh)
+
+        def pick_second(s):
+            second[s] = ring.tile([P, PAIRS], F32, name="second", tag="second")
+            nc.vector.tensor_copy(second[s][:], h[s][:].indirect(pos2_sb[:]))
+
+        def differences(s):
+            a1[s] = ring.tile([P, PAIRS], F32, name="a1", tag="a1", align_bytes=64)
+            nc.vector.tensor_tensor(a1[s][:], h[s][:].indirect(pos1_sb[:]), second[s][:], ALU.subtract)
+
+        def kept_pairs(s, j0, j1):
+            g, t = divmod(s, PACK)
+            nc.vector.tensor_tensor(
+                a2[g][:, t, j0:j1], a1[s][:].indirect(pos3_sb[:, j0 // 16 : j1 // 16]), view[(s, j0)][:], ALU.mult
+            )
+            nc.scalar.activation(x_bf[g][:, j0:j1, t], a2[g][:, t, j0:j1], ACT.Copy, scale=gain_sb[:, g, t : t + 1])
+
+        def quantise_x(g, j0, j1):
+            nc.vector.quantize_mx(
+                out=x_q[g][:, j0:j1].bitcast(FP8X4), scales=x_s[g][:, j0:j1],
+                in_=x_bf[g][:, j0:j1, :].rearrange("p j t -> p (j t)"),
+            )
+
+        wo_q = [keep.tile([P, N], I32, name="wo_q%d" % a, align_bytes=64) for a in range(GROUPS)]
+
+        def deal_wo(a):
+            nc.vector.tensor_copy(
+                wo_q[a][:].rearrange("p (g t m i) -> p g m t i", g=GROUPS, t=PACK, i=4),
+                wo_raw[a][:].rearrange("p (g m i t) -> p g m t i", g=GROUPS, t=PACK, i=4),
+            )
+
+        round_weight(0, 0)
+        quantise_weight(0, 0)
+        round_weight(1, 0)
+        first_max(0, 0)
+        first_max(0, 1)
+        quantise_weight(1, 0)
+        second_max(0, 0)
+        second_max(0, 1)
+        for s in range(SLICES - 1):
+            ahead = s + 2
+            if ahead % 2 == 0 and ahead < SLICES:
+                round_weight(0, ahead)
+                round_weight(1, ahead)
+            pick_view(s, 0, KEPT)
+            pick_second(s)
+            first_max(s + 1, 0)
+            differences(s)
+            first_max(s + 1, 1)
+            if ahead % 2 == 0 and ahead < SLICES:
+                quantise_weight(0, ahead)
+                quantise_weight(1, ahead)
+            if s == PACK:
+                quantise_x(0, 0, KEPT)
+            if s in (PACK - 1, PACK + 1):
+                deal_wo((s - PACK + 1) // 2)
+            second_max(s + 1, 0)
+            second_max(s + 1, 1)
+            kept_pairs(s, 0, KEPT)
+
+        y_acc = {}
+        for c in range(HALVES):
+            for g in range(GROUPS):
+                tag, bufs = (("acc2", 2), ("acc1", 3))[c]
+                y_acc[(g, c)] = psum.tile([P, PACK, KEPT_HALF], F32, name="y_acc", tag=tag, bufs=bufs)
+
+        def y_passes(a, g, c):
+            kept = slice(c * KEPT_HALF, (c + 1) * KEPT_HALF)
+            for t in range(PACK):
+                cols = slice(g * GROUP + t * P, g * GROUP + (t + 1) * P)
+                nc.tensor.matmul_mx(
+                    out=y_acc[(g, c)][:, t, :],
+                    lhsT=wo_q[a][:, cols].bitcast(FP8X4), lhsT_scale=w_s[4 * (a + 1) :, cols],
+                    rhs=x_q[a][:, kept].bitcast(FP8X4), rhs_scale=x_s[a][:, kept],
+                    start=(a == 0 and t == 0), stop=(a == GROUPS - 1 and t == PACK - 1),
+                )
+
+        for c in range(HALVES):
+            for g in range(GROUPS):
+                y_passes(0, g, c)
+
+        last = SLICES - 1
+        pick_second(last)
+        pick_view(last, 0, KEPT_HALF)
+        differences(last)
+        pick_view(last, KEPT_HALF, KEPT)
+        for c in range(HALVES):
+            kept_pairs(last, c * KEPT_HALF, (c + 1) * KEPT_HALF)
+        for c in range(HALVES):
+            quantise_x(1, c * KEPT_HALF, (c + 1) * KEPT_HALF)
+            for g in range(GROUPS):
+                y_passes(1, g, c)
+
+        y_s = keep.tile([P, GROUPS, KEPT], U8, name="y_s", align_bytes=64)
+        y_bf = {}
+
+        def finish(g, c):
+            kept = slice(c * KEPT_HALF, (c + 1) * KEPT_HALF)
+            y = keep.tile([P, PACK, KEPT_HALF], F32, name="y%d%d" % (g, c), align_bytes=64)
+            nc.vector.tensor_tensor(y[:], y_acc[(g, c)][:], a2[g][:, :, kept], ALU.add)
+            nc.sync.dma_start(out_0[g * GROUP : (g + 1) * GROUP, kept].rearrange("(p t) j -> p t j", t=PACK), y[:])
+            y_bf[(g, c)] = keep.tile([P, KEPT_HALF, PACK], BF16, name="y_bf%d%d" % (g, c), align_bytes=64)
+            nc.scalar.copy(
+                y_bf[(g, c)][:].rearrange("p (j i) t -> p j t i", i=4),
+                y[:].rearrange("p t (j i) -> p j t i", i=4),
+            )
+
+        def planes(g, c):
+            kept = slice(c * KEPT_HALF, (c + 1) * KEPT_HALF)
+            y_q = keep.tile([P, KEPT_HALF], I32, name="y_q%d%d" % (g, c), align_bytes=64)
+            nc.vector.quantize_mx(
+                out=y_q[:].bitcast(FP8X4), scales=y_s[:, g, kept],
+                in_=y_bf[(g, c)][:].rearrange("p j t -> p (j t)"),
+            )
+            nc.sync.dma_start(out_1[g, :, kept, :].rearrange("p m t -> p (m t)").bitcast(I32), y_q[:])
+
+        order = [(g, c) for c in range(HALVES) for g in range(GROUPS)]
+        for n, (g, c) in enumerate(order):
+            finish(g, c)
+            if n >= 2:
+                planes(*order[n - 2])
+        for g, c in order[-2:]:
+            planes(g, c)
+        for q in range(QUADS):
+            queue = (nc.sync, nc.scalar)[q % 2]
+            queue.dma_start(
+                out_2[:, 4 * q : 4 * q + 4, :].rearrange("g r m -> r g m").bitcast(I32),
+                y_s[32 * q : 32 * q + 4, :, :].bitcast(I32),
+            )

@@ -42,55 +42,49 @@ def tile_list_footage_pair_features_kernel(
             nc.sync.dma_start(lst[:], src)
             return lst
 
-        offs_sb = load_list(offs, "offs_sb")
-        tab_s = keep.tile([P, T], U8, name="tab_s", align_bytes=64)
-        nc.vector.memset(tab_s[:].bitcast(I32), 0)
-        w_s_raw = keep.tile([P, H], U8, name="w_s_raw", align_bytes=64)
-        nc.vector.memset(w_s_raw[:].bitcast(I32), 0)
-        for q in range(QUADS):
-            nc.sync.dma_start(tab_s[32 * q : 32 * q + 4, :].bitcast(I32), tab_scales[0, 4 * q : 4 * q + 4, :].bitcast(I32))
-        tab_w = keep.tile([P, T], I32, name="tab_w", align_bytes=64)
-        nc.sync.dma_start(tab_w[:], tab_words[0].rearrange("p t i -> p (t i)").bitcast(I32))
-        w2_raw = keep.tile([P, H], U16, name="w2_raw", align_bytes=64)
-        nc.scalar.dma_start(w2_raw[:].bitcast(I32), w2_words[0].bitcast(I32))
-
-        def load_weight(w, g, name):
-            raw = keep.tile([P, PACK, GROUP], F32, name=name, align_bytes=64)
+        def load_weight(w, g, tag):
+            raw = keep.tile([P, PACK, GROUP], F32, name=tag, tag=tag, align_bytes=64)
             nc.sync.dma_start(raw[:], w[:, g * GROUP : (g + 1) * GROUP].rearrange("(p j) c -> p j c", j=PACK))
             return raw
 
-        w_raw = {}
-        w_raw[(0, 0)] = load_weight(w1, 0, "w1_raw0")
-        for q in range(QUADS):
-            nc.scalar.dma_start(w_s_raw[32 * q : 32 * q + 4, :].bitcast(I32), w2_scales[0, 4 * q : 4 * q + 4, :].bitcast(I32))
-            nc.gpsimd.dma_start(w_s_raw[32 * q + 4 : 32 * q + 12, :].bitcast(I32), wo_scales[:, 4 * q : 4 * q + 4, :].bitcast(I32))
-        w_raw[(1, 0)] = load_weight(w3, 0, "w3_raw0")
+        def deal_columns(name, raw):
+            dealt = keep.tile(list(raw.shape), raw.dtype, name=name, align_bytes=64)
+            nc.vector.tensor_copy(
+                dealt[:].rearrange("p (g t m) -> p g t m", g=GROUPS, t=PACK),
+                raw[:].rearrange("p (g m t) -> p g t m", g=GROUPS, t=PACK),
+            )
+            return dealt
+
+        tab_s = keep.tile([P, T], U8, name="tab_s", align_bytes=64)
+        nc.vector.memset(tab_s[:].bitcast(I32), 0)
+        w2_s_raw = keep.tile([P, H], U8, name="w2_s_raw", tag="scales_raw", align_bytes=64)
+        nc.gpsimd.memset(w2_s_raw[:].bitcast(I32), 0)
+        offs_sb = load_list(offs, "offs_sb")
+        w2_raw = keep.tile([P, H], U16, name="w2_raw", align_bytes=64)
+        nc.scalar.dma_start(w2_raw[:].bitcast(I32), w2_words[0].bitcast(I32))
         pos4_sb = load_list(pos4, "pos4_sb")
         pos2_sb = load_list(pos2, "pos2_sb")
         pos1_sb = load_list(pos1, "pos1_sb")
         pos3_sb = load_list(pos3, "pos3_sb")
         gain_sb = keep.tile([P, GROUPS, PACK], F32, name="gain_sb")
         nc.sync.dma_start(gain_sb[:], gain.rearrange("(g p t) -> p g t", g=GROUPS, t=PACK))
-        w_raw[(0, 1)] = load_weight(w1, 1, "w1_raw1")
-        w_raw[(1, 1)] = load_weight(w3, 1, "w3_raw1")
-        wo_raw = []
-        for a in range(GROUPS):
-            raw = keep.tile([P, N], I32, name="wo_raw%d" % a, align_bytes=64)
-            nc.sync.dma_start(raw[:], wo_words[a].rearrange("p c i -> p (c i)").bitcast(I32))
-            wo_raw.append(raw)
+        w_raw = {}
+        w_raw[(0, 0)] = load_weight(w1, 0, "w1_raw")
+        tab_w = keep.tile([P, T], I32, name="tab_w", align_bytes=64)
+        nc.sync.dma_start(tab_w[:], tab_words[0].rearrange("p t i -> p (t i)").bitcast(I32))
+        w_raw[(1, 0)] = load_weight(w3, 0, "w3_raw")
+        for q in range(QUADS):
+            nc.scalar.dma_start(tab_s[32 * q : 32 * q + 4, :].bitcast(I32), tab_scales[0, 4 * q : 4 * q + 4, :].bitcast(I32))
+            nc.gpsimd.dma_start(w2_s_raw[32 * q : 32 * q + 4, :].bitcast(I32), w2_scales[0, 4 * q : 4 * q + 4, :].bitcast(I32))
 
+        w2_q = deal_columns("w2_q", w2_raw)
         v_s = keep.tile([P, S], U8, name="v_s", align_bytes=64)
         nc.vector.tensor_copy(v_s[:], tab_s[:].indirect(offs_sb[:]))
-        w2_q = keep.tile([P, H], U16, name="w2_q", align_bytes=64)
-        nc.vector.tensor_copy(
-            w2_q[:].rearrange("p (g t m) -> p g t m", g=GROUPS, t=PACK),
-            w2_raw[:].rearrange("p (g m t) -> p g t m", g=GROUPS, t=PACK),
-        )
-        w_s = keep.tile([P, H], U8, name="w_s", align_bytes=64)
-        nc.vector.tensor_copy(
-            w_s[:].rearrange("p (g t m) -> p g t m", g=GROUPS, t=PACK),
-            w_s_raw[:].rearrange("p (g m t) -> p g t m", g=GROUPS, t=PACK),
-        )
+        w2_s = deal_columns("w2_s", w2_s_raw)
+        wo_s_raw = keep.tile([P, N], U8, name="wo_s_raw", tag="scales_raw", align_bytes=64)
+        nc.gpsimd.memset(wo_s_raw[:].bitcast(I32), 0)
+        for q in range(QUADS):
+            nc.sync.dma_start(wo_s_raw[32 * q : 32 * q + 8, :].bitcast(I32), wo_scales[:, 4 * q : 4 * q + 4, :].bitcast(I32))
         v_w = keep.tile([P, S], U32, name="v_w", align_bytes=64)
         for c in range(HALVES):
             nc.vector.tensor_copy(
@@ -131,7 +125,7 @@ def tile_list_footage_pair_features_kernel(
         h = {}
 
         def first_max(s, c):
-            acc2 = product("acc2", 2, lambda cols: w2_q[:, cols].bitcast(FP4X4), w_s, s, c)
+            acc2 = product("acc2", 2, lambda cols: w2_q[:, cols].bitcast(FP4X4), w2_s, s, c)
             acc1 = product("acc1", 3, lambda cols: w_q[0][:, cols].bitcast(FP8X4), w_qs[0], s, c)
             sum2 = ring.tile([P, BANK], F32, name="sum2", tag="sum2", bufs=4)
             nc.scalar.copy(sum2[:], acc2[:])
@@ -181,10 +175,10 @@ def tile_list_footage_pair_features_kernel(
 
         wo_q = [keep.tile([P, N], I32, name="wo_q%d" % a, align_bytes=64) for a in range(GROUPS)]
 
-        def deal_wo(a):
+        def deal_wo(wo_raw, a):
             nc.vector.tensor_copy(
                 wo_q[a][:].rearrange("p (g t m i) -> p g m t i", g=GROUPS, t=PACK, i=4),
-                wo_raw[a][:].rearrange("p (g m i t) -> p g m t i", g=GROUPS, t=PACK, i=4),
+                wo_raw[:, a, :].rearrange("p (g m i t) -> p g m t i", g=GROUPS, t=PACK, i=4),
             )
 
         round_weight(0, 0)
@@ -200,6 +194,12 @@ def tile_list_footage_pair_features_kernel(
             if ahead % 2 == 0 and ahead < SLICES:
                 round_weight(0, ahead)
                 round_weight(1, ahead)
+                if ahead == PACK - 2:
+                    w_raw[(0, 1)] = load_weight(w1, 1, "w1_raw")
+                    w_raw[(1, 1)] = load_weight(w3, 1, "w3_raw")
+                if ahead == SLICES - 2:
+                    wo_raw = keep.tile([P, GROUPS, N], I32, name="wo_raw", tag="w1_raw", align_bytes=64)
+                    nc.sync.dma_start(wo_raw[:], wo_words.rearrange("a p c i -> p a (c i)").bitcast(I32))
             pick_view(s, 0, KEPT)
             pick_second(s)
             first_max(s + 1, 0)
@@ -210,8 +210,9 @@ def tile_list_footage_pair_features_kernel(
                 quantise_weight(1, ahead)
             if s == PACK:
                 quantise_x(0, 0, KEPT)
-            if s in (PACK - 1, PACK + 1):
-                deal_wo((s - PACK + 1) // 2)
+                wo_s = deal_columns("wo_s", wo_s_raw)
+            if s > PACK:
+                deal_wo(wo_raw, s - PACK - 1)
             second_max(s + 1, 0)
             second_max(s + 1, 1)
             kept_pairs(s, 0, KEPT)
@@ -228,7 +229,7 @@ def tile_list_footage_pair_features_kernel(
                 cols = slice(g * GROUP + t * P, g * GROUP + (t + 1) * P)
                 nc.tensor.matmul_mx(
                     out=y_acc[(g, c)][:, t, :],
-                    lhsT=wo_q[a][:, cols].bitcast(FP8X4), lhsT_scale=w_s[4 * (a + 1) :, cols],
+                    lhsT=wo_q[a][:, cols].bitcast(FP8X4), lhsT_scale=wo_s[4 * a :, cols],
                     rhs=x_q[a][:, kept].bitcast(FP8X4), rhs_scale=x_s[a][:, kept],
                     start=(a == 0 and t == 0), stop=(a == GROUPS - 1 and t == PACK - 1),
                 )

@@ -47,9 +47,9 @@ def tile_list_footage_pair_features_kernel(
             nc.sync.dma_start(raw[:], w[:, g * GROUP : (g + 1) * GROUP].rearrange("(p j) c -> p j c", j=PACK))
             return raw
 
-        def deal_columns(name, raw):
+        def deal_columns(name, raw, engine):
             dealt = keep.tile(list(raw.shape), raw.dtype, name=name, align_bytes=64)
-            nc.vector.tensor_copy(
+            engine.tensor_copy(
                 dealt[:].rearrange("p (g t m) -> p g t m", g=GROUPS, t=PACK),
                 raw[:].rearrange("p (g m t) -> p g t m", g=GROUPS, t=PACK),
             )
@@ -61,26 +61,27 @@ def tile_list_footage_pair_features_kernel(
         nc.gpsimd.memset(w2_s_raw[:].bitcast(I32), 0)
         offs_sb = load_list(offs, "offs_sb")
         w2_raw = keep.tile([P, H], U16, name="w2_raw", align_bytes=64)
-        nc.scalar.dma_start(w2_raw[:].bitcast(I32), w2_words[0].bitcast(I32))
+        nc.sync.dma_start(w2_raw[:].bitcast(I32), w2_words[0].bitcast(I32))
         pos4_sb = load_list(pos4, "pos4_sb")
         pos2_sb = load_list(pos2, "pos2_sb")
         pos1_sb = load_list(pos1, "pos1_sb")
+        w_raw = {}
+        w_raw[(0, 0)] = load_weight(w1, 0, "w1_raw")
         pos3_sb = load_list(pos3, "pos3_sb")
         gain_sb = keep.tile([P, GROUPS, PACK], F32, name="gain_sb")
         nc.sync.dma_start(gain_sb[:], gain.rearrange("(g p t) -> p g t", g=GROUPS, t=PACK))
-        w_raw = {}
-        w_raw[(0, 0)] = load_weight(w1, 0, "w1_raw")
-        tab_w = keep.tile([P, T], I32, name="tab_w", align_bytes=64)
-        nc.sync.dma_start(tab_w[:], tab_words[0].rearrange("p t i -> p (t i)").bitcast(I32))
-        w_raw[(1, 0)] = load_weight(w3, 0, "w3_raw")
         for q in range(QUADS):
-            nc.scalar.dma_start(tab_s[32 * q : 32 * q + 4, :].bitcast(I32), tab_scales[0, 4 * q : 4 * q + 4, :].bitcast(I32))
-            nc.gpsimd.dma_start(w2_s_raw[32 * q : 32 * q + 4, :].bitcast(I32), w2_scales[0, 4 * q : 4 * q + 4, :].bitcast(I32))
+            nc.sync.dma_start(tab_s[32 * q : 32 * q + 4, :].bitcast(I32), tab_scales[0, 4 * q : 4 * q + 4, :].bitcast(I32))
+        tab_w = keep.tile([P, T], I32, name="tab_w", tag="tab_w", align_bytes=64)
+        nc.sync.dma_start(tab_w[:], tab_words[0].rearrange("p t i -> p (t i)").bitcast(I32))
+        for q in range(QUADS):
+            nc.sync.dma_start(w2_s_raw[32 * q : 32 * q + 4, :].bitcast(I32), w2_scales[0, 4 * q : 4 * q + 4, :].bitcast(I32))
+        w_raw[(1, 0)] = load_weight(w3, 0, "w3_raw")
 
-        w2_q = deal_columns("w2_q", w2_raw)
+        w2_q = deal_columns("w2_q", w2_raw, nc.vector)
         v_s = keep.tile([P, S], U8, name="v_s", align_bytes=64)
         nc.vector.tensor_copy(v_s[:], tab_s[:].indirect(offs_sb[:]))
-        w2_s = deal_columns("w2_s", w2_s_raw)
+        w2_s = deal_columns("w2_s", w2_s_raw, nc.vector)
         wo_s_raw = keep.tile([P, N], U8, name="wo_s_raw", tag="scales_raw", align_bytes=64)
         nc.gpsimd.memset(wo_s_raw[:].bitcast(I32), 0)
         for q in range(QUADS):
@@ -91,6 +92,9 @@ def tile_list_footage_pair_features_kernel(
                 v_w[:, c * BANK : (c + 1) * BANK],
                 tab_w[:].bitcast(U32).indirect(offs_sb[:, c * BANK // 16 : (c + 1) * BANK // 16]),
             )
+
+        wo_raw = keep.tile([P, GROUPS, N], I32, name="wo_raw", tag="tab_w", align_bytes=64)
+        nc.sync.dma_start(wo_raw[:], wo_words.rearrange("a p c i -> p a (c i)").bitcast(I32))
 
         w_q = [keep.tile([P, H], U32, name="w_q%d" % i, align_bytes=64) for i in range(2)]
         w_qs = [keep.tile([P, H], U8, name="w_qs%d" % i, align_bytes=64) for i in range(2)]
@@ -125,12 +129,12 @@ def tile_list_footage_pair_features_kernel(
         h = {}
 
         def first_max(s, c):
-            acc2 = product("acc2", 2, lambda cols: w2_q[:, cols].bitcast(FP4X4), w2_s, s, c)
-            acc1 = product("acc1", 3, lambda cols: w_q[0][:, cols].bitcast(FP8X4), w_qs[0], s, c)
-            sum2 = ring.tile([P, BANK], F32, name="sum2", tag="sum2", bufs=4)
-            nc.scalar.copy(sum2[:], acc2[:])
-            h12[(s, c)] = ring.tile([P, BANK], F32, name="h12", tag="h12", bufs=6)
-            nc.vector.tensor_tensor(h12[(s, c)][:], acc1[:], sum2[:], ALU.max)
+            acc1 = product("acc1", 2, lambda cols: w_q[0][:, cols].bitcast(FP8X4), w_qs[0], s, c)
+            acc2 = product("acc2", 3, lambda cols: w2_q[:, cols].bitcast(FP4X4), w2_s, s, c)
+            sum1 = ring.tile([P, BANK], F32, name="sum1", tag="sum1", bufs=4)
+            nc.scalar.copy(sum1[:], acc1[:])
+            h12[(s, c)] = ring.tile([P, BANK], F32, name="h12", tag="h12", bufs=8)
+            nc.vector.tensor_tensor(h12[(s, c)][:], acc2[:], sum1[:], ALU.max)
 
         def second_max(s, c):
             acc3 = product("acc3", 3, lambda cols: w_q[1][:, cols].bitcast(FP8X4), w_qs[1], s, c)
@@ -138,7 +142,9 @@ def tile_list_footage_pair_features_kernel(
                 h[s] = ring.tile([P, S], F32, name="h", tag="h", bufs=2, align_bytes=64)
             nc.vector.tensor_tensor(h[s][:, c * BANK : (c + 1) * BANK], acc3[:], h12[(s, c)][:], ALU.max)
 
-        a2 = [keep.tile([P, PACK, KEPT], F32, name="a2_%d" % g, align_bytes=64) for g in range(GROUPS)]
+        a2_first = keep.tile([P, PACK, KEPT], F32, name="a2_first", align_bytes=64)
+        a2 = {(0, c): a2_first[:, :, c * KEPT_HALF : (c + 1) * KEPT_HALF] for c in range(HALVES)}
+        a2[(1, 0)] = keep.tile([P, PACK, KEPT_HALF], F32, name="a2_early", align_bytes=64)[:]
         x_bf = [keep.tile([P, KEPT, PACK], BF16, name="x_bf%d" % g, align_bytes=64) for g in range(GROUPS)]
         x_q = [keep.tile([P, KEPT], U32, name="x_q%d" % g, align_bytes=64) for g in range(GROUPS)]
         x_s = [keep.tile([P, KEPT], U8, name="x_s%d" % g, align_bytes=64) for g in range(GROUPS)]
@@ -146,26 +152,28 @@ def tile_list_footage_pair_features_kernel(
         second = {}
         a1 = {}
 
-        def pick_view(s, j0, j1):
-            picked = ring.tile([P, j1 - j0], F32, name="picked4", tag="picked4")
-            nc.vector.tensor_copy(picked[:], h[s][:].indirect(pos4_sb[:, j0 // 16 : j1 // 16]))
-            view[(s, j0)] = ring.tile([P, j1 - j0], F32, name="view", tag="view")
-            nc.scalar.activation(view[(s, j0)][:], picked[:], ACT.Tanh)
+        def pick_view(s):
+            picked = ring.tile([P, KEPT], F32, name="picked4", tag="picked4")
+            nc.vector.tensor_copy(picked[:], h[s][:].indirect(pos4_sb[:]))
+            view[s] = ring.tile([P, KEPT], F32, name="view", tag="view", bufs=PACK + 1)
+            nc.scalar.activation(view[s][:], picked[:], ACT.Tanh)
 
         def pick_second(s):
-            second[s] = ring.tile([P, PAIRS], F32, name="second", tag="second")
+            second[s] = ring.tile([P, PAIRS], F32, name="second", tag="second", bufs=1, align_bytes=64)
             nc.vector.tensor_copy(second[s][:], h[s][:].indirect(pos2_sb[:]))
 
         def differences(s):
-            a1[s] = ring.tile([P, PAIRS], F32, name="a1", tag="a1", align_bytes=64)
+            a1[s] = ring.tile([P, PAIRS], F32, name="a1", tag="a1", bufs=PACK + 1, align_bytes=64)
             nc.vector.tensor_tensor(a1[s][:], h[s][:].indirect(pos1_sb[:]), second[s][:], ALU.subtract)
 
-        def kept_pairs(s, j0, j1):
+        def kept_pairs(s, dst, j0, j1):
             g, t = divmod(s, PACK)
-            nc.vector.tensor_tensor(
-                a2[g][:, t, j0:j1], a1[s][:].indirect(pos3_sb[:, j0 // 16 : j1 // 16]), view[(s, j0)][:], ALU.mult
-            )
-            nc.scalar.activation(x_bf[g][:, j0:j1, t], a2[g][:, t, j0:j1], ACT.Copy, scale=gain_sb[:, g, t : t + 1])
+            nc.vector.tensor_tensor(dst, a1[s][:].indirect(pos3_sb[:, j0 // 16 : j1 // 16]), view[s][:, j0:j1], ALU.mult)
+            nc.scalar.activation(x_bf[g][:, j0:j1, t], dst, ACT.Copy, scale=gain_sb[:, g, t : t + 1])
+
+        def kept_half(s, c):
+            g, t = divmod(s, PACK)
+            kept_pairs(s, a2[(g, c)][:, t, :], c * KEPT_HALF, (c + 1) * KEPT_HALF)
 
         def quantise_x(g, j0, j1):
             nc.vector.quantize_mx(
@@ -175,11 +183,18 @@ def tile_list_footage_pair_features_kernel(
 
         wo_q = [keep.tile([P, N], I32, name="wo_q%d" % a, align_bytes=64) for a in range(GROUPS)]
 
-        def deal_wo(wo_raw, a):
-            nc.vector.tensor_copy(
-                wo_q[a][:].rearrange("p (g t m i) -> p g m t i", g=GROUPS, t=PACK, i=4),
-                wo_raw[:, a, :].rearrange("p (g m i t) -> p g m t i", g=GROUPS, t=PACK, i=4),
-            )
+        wo_s = keep.tile([P, N], U8, name="wo_s", align_bytes=64)
+        for g in range(GROUPS):
+            group = slice(g * GROUP, (g + 1) * GROUP)
+            for t in range(0, PACK, 2):
+                cols = slice(g * GROUP + t * P, g * GROUP + (t + 2) * P)
+                moves = [(wo_q[a][:, cols], wo_raw[:, a, group]) for a in range(GROUPS)]
+                moves.append((wo_s[:, cols], wo_s_raw[:, group]))
+                for dst, src in moves:
+                    nc.gpsimd.tensor_copy(
+                        dst.rearrange("p (t m) -> p t m", t=2),
+                        src.rearrange("p (m t) -> p t m", t=PACK)[:, t : t + 2, :],
+                    )
 
         round_weight(0, 0)
         quantise_weight(0, 0)
@@ -197,10 +212,7 @@ def tile_list_footage_pair_features_kernel(
                 if ahead == PACK - 2:
                     w_raw[(0, 1)] = load_weight(w1, 1, "w1_raw")
                     w_raw[(1, 1)] = load_weight(w3, 1, "w3_raw")
-                if ahead == SLICES - 2:
-                    wo_raw = keep.tile([P, GROUPS, N], I32, name="wo_raw", tag="w1_raw", align_bytes=64)
-                    nc.sync.dma_start(wo_raw[:], wo_words.rearrange("a p c i -> p a (c i)").bitcast(I32))
-            pick_view(s, 0, KEPT)
+            pick_view(s)
             pick_second(s)
             first_max(s + 1, 0)
             differences(s)
@@ -210,17 +222,17 @@ def tile_list_footage_pair_features_kernel(
                 quantise_weight(1, ahead)
             if s == PACK:
                 quantise_x(0, 0, KEPT)
-                wo_s = deal_columns("wo_s", wo_s_raw)
-            if s > PACK:
-                deal_wo(wo_raw, s - PACK - 1)
             second_max(s + 1, 0)
             second_max(s + 1, 1)
-            kept_pairs(s, 0, KEPT)
+            if s < PACK:
+                kept_pairs(s, a2_first[:, s, :], 0, KEPT)
+            else:
+                kept_half(s, 0)
 
         y_acc = {}
         for c in range(HALVES):
             for g in range(GROUPS):
-                tag, bufs = (("acc2", 2), ("acc1", 3))[c]
+                tag, bufs = (("acc1", 2), ("acc2", 3))[c]
                 y_acc[(g, c)] = psum.tile([P, PACK, KEPT_HALF], F32, name="y_acc", tag=tag, bufs=bufs)
 
         def y_passes(a, g, c):
@@ -240,15 +252,17 @@ def tile_list_footage_pair_features_kernel(
 
         last = SLICES - 1
         pick_second(last)
-        pick_view(last, 0, KEPT_HALF)
+        pick_view(last)
         differences(last)
-        pick_view(last, KEPT_HALF, KEPT)
-        for c in range(HALVES):
-            kept_pairs(last, c * KEPT_HALF, (c + 1) * KEPT_HALF)
-        for c in range(HALVES):
-            quantise_x(1, c * KEPT_HALF, (c + 1) * KEPT_HALF)
-            for g in range(GROUPS):
-                y_passes(1, g, c)
+        a2[(1, 1)] = ring.tile([P, PACK, KEPT_HALF], F32, name="a2_late", tag="second", bufs=1, align_bytes=64)[:]
+        kept_half(PACK, 1)
+        kept_half(last, 0)
+        kept_half(PACK + 1, 1)
+        kept_half(PACK + 2, 1)
+        quantise_x(1, 0, KEPT_HALF)
+        for g in range(GROUPS):
+            y_passes(1, g, 0)
+        kept_half(last, 1)
 
         y_s = keep.tile([P, GROUPS, KEPT], U8, name="y_s", align_bytes=64)
         y_bf = {}
@@ -256,7 +270,7 @@ def tile_list_footage_pair_features_kernel(
         def finish(g, c):
             kept = slice(c * KEPT_HALF, (c + 1) * KEPT_HALF)
             y = keep.tile([P, PACK, KEPT_HALF], F32, name="y%d%d" % (g, c), align_bytes=64)
-            nc.vector.tensor_tensor(y[:], y_acc[(g, c)][:], a2[g][:, :, kept], ALU.add)
+            nc.vector.tensor_tensor(y[:], y_acc[(g, c)][:], a2[(g, c)], ALU.add)
             nc.sync.dma_start(out_0[g * GROUP : (g + 1) * GROUP, kept].rearrange("(p t) j -> p t j", t=PACK), y[:])
             y_bf[(g, c)] = keep.tile([P, KEPT_HALF, PACK], BF16, name="y_bf%d%d" % (g, c), align_bytes=64)
             nc.scalar.copy(
@@ -276,6 +290,10 @@ def tile_list_footage_pair_features_kernel(
         order = [(g, c) for c in range(HALVES) for g in range(GROUPS)]
         for n, (g, c) in enumerate(order):
             finish(g, c)
+            if n == 0:
+                quantise_x(1, KEPT_HALF, KEPT)
+                for late in range(GROUPS):
+                    y_passes(1, late, 1)
             if n >= 2:
                 planes(*order[n - 2])
         for g, c in order[-2:]:

@@ -25,6 +25,7 @@ BANK = 512
 HALVES = 2
 KEPT_HALF = KEPT // HALVES
 QUADS = 4
+CLEAR_SPLIT = 2816
 
 
 def tile_list_footage_pair_features_kernel(
@@ -42,58 +43,62 @@ def tile_list_footage_pair_features_kernel(
             nc.sync.dma_start(lst[:], src)
             return lst
 
-        def load_weight(w, g, tag):
-            raw = keep.tile([P, PACK, GROUP], F32, name=tag, tag=tag, align_bytes=64)
-            nc.sync.dma_start(raw[:], w[:, g * GROUP : (g + 1) * GROUP].rearrange("(p j) c -> p j c", j=PACK))
-            return raw
+        def load_weight(w, g, tags):
+            width = GROUP // len(tags)
+            pieces = []
+            for n, tag in enumerate(tags):
+                raw = keep.tile([P, PACK, width], F32, name=tag, tag=tag, align_bytes=64)
+                cols = slice(g * GROUP + n * width, g * GROUP + (n + 1) * width)
+                nc.sync.dma_start(raw[:], w[:, cols].rearrange("(p j) c -> p j c", j=PACK))
+                pieces.append(raw)
+            return pieces
 
-        def deal_columns(name, raw, engine):
-            dealt = keep.tile(list(raw.shape), raw.dtype, name=name, align_bytes=64)
-            engine.tensor_copy(
-                dealt[:].rearrange("p (g t m) -> p g t m", g=GROUPS, t=PACK),
-                raw[:].rearrange("p (g m t) -> p g t m", g=GROUPS, t=PACK),
+        def deal_columns(tag, raw, run):
+            dealt = keep.tile(list(raw.shape), raw.dtype, name="dealt", tag=tag, align_bytes=64)
+            nc.vector.tensor_copy(
+                dealt[:].rearrange("p (g t m i) -> p g m t i", g=GROUPS, t=PACK, i=run),
+                raw.rearrange("p (g m i t) -> p g m t i", g=GROUPS, t=PACK, i=run),
             )
             return dealt
 
-        tab_s = keep.tile([P, T], U8, name="tab_s", align_bytes=64)
-        nc.vector.memset(tab_s[:].bitcast(I32), 0)
+        tab_s = keep.tile([P, T], U8, name="tab_s", tag="w3_raw", align_bytes=64)
+        nc.vector.memset(tab_s[:, :CLEAR_SPLIT].bitcast(I32), 0)
+        nc.gpsimd.memset(tab_s[:, CLEAR_SPLIT:].bitcast(I32), 0)
         w2_s_raw = keep.tile([P, H], U8, name="w2_s_raw", tag="scales_raw", align_bytes=64)
         nc.gpsimd.memset(w2_s_raw[:].bitcast(I32), 0)
+        v_s = keep.tile([P, S], U8, name="v_s", align_bytes=64)
+        nc.vector.memset(v_s[:].bitcast(I32), 0)
         offs_sb = load_list(offs, "offs_sb")
         w2_raw = keep.tile([P, H], U16, name="w2_raw", align_bytes=64)
         nc.sync.dma_start(w2_raw[:].bitcast(I32), w2_words[0].bitcast(I32))
         pos4_sb = load_list(pos4, "pos4_sb")
         pos2_sb = load_list(pos2, "pos2_sb")
         pos1_sb = load_list(pos1, "pos1_sb")
-        w_raw = {}
-        w_raw[(0, 0)] = load_weight(w1, 0, "w1_raw")
         pos3_sb = load_list(pos3, "pos3_sb")
+        nc.sync.dma_start(tab_s[0:P:8, :].bitcast(I32), tab_scales[0].bitcast(I32))
+        tab_w = keep.tile([P, T], I32, name="tab_w", tag="tab_w", align_bytes=64)
+        nc.sync.dma_start(tab_w[:], tab_words[0].rearrange("p t i -> p (t i)").bitcast(I32))
+        w_raw = {}
+        w_raw[(0, 0)] = load_weight(w1, 0, ["w1_raw_a", "w1_raw_b"])
         gain_sb = keep.tile([P, GROUPS, PACK], F32, name="gain_sb")
         nc.sync.dma_start(gain_sb[:], gain.rearrange("(g p t) -> p g t", g=GROUPS, t=PACK))
         for q in range(QUADS):
-            nc.sync.dma_start(tab_s[32 * q : 32 * q + 4, :].bitcast(I32), tab_scales[0, 4 * q : 4 * q + 4, :].bitcast(I32))
-        tab_w = keep.tile([P, T], I32, name="tab_w", tag="tab_w", align_bytes=64)
-        nc.sync.dma_start(tab_w[:], tab_words[0].rearrange("p t i -> p (t i)").bitcast(I32))
-        for q in range(QUADS):
-            nc.sync.dma_start(w2_s_raw[32 * q : 32 * q + 4, :].bitcast(I32), w2_scales[0, 4 * q : 4 * q + 4, :].bitcast(I32))
-        w_raw[(1, 0)] = load_weight(w3, 0, "w3_raw")
+            nc.gpsimd.dma_start(w2_s_raw[32 * q : 32 * q + 4, :].bitcast(I32), w2_scales[0, 4 * q : 4 * q + 4, :].bitcast(I32))
 
-        w2_q = deal_columns("w2_q", w2_raw, nc.vector)
-        v_s = keep.tile([P, S], U8, name="v_s", align_bytes=64)
-        nc.vector.tensor_copy(v_s[:], tab_s[:].indirect(offs_sb[:]))
-        w2_s = deal_columns("w2_s", w2_s_raw, nc.vector)
+        w2_q = deal_columns("w2_q", w2_raw[:], 8)
+        picked_s = keep.tile([P, S], U8, name="picked_s", tag="picked_s", align_bytes=64)
+        nc.vector.tensor_copy(picked_s[:], tab_s[:].indirect(offs_sb[:]))
+        for q in range(QUADS):
+            nc.sync.dma_start(v_s[32 * q : 32 * q + 4, :].bitcast(I32), picked_s[32 * q : 32 * (q + 1) : 8, :].bitcast(I32))
+        w_raw[(1, 0)] = load_weight(w3, 0, ["w3_raw"])
+        v_w = keep.tile([P, S], U32, name="v_w", align_bytes=64)
+        nc.vector.tensor_copy(v_w[:], tab_w[:].bitcast(U32).indirect(offs_sb[:]))
+        w2_s = deal_columns("tab_w", w2_s_raw[:], 16)
         wo_s_raw = keep.tile([P, N], U8, name="wo_s_raw", tag="scales_raw", align_bytes=64)
         nc.gpsimd.memset(wo_s_raw[:].bitcast(I32), 0)
         for q in range(QUADS):
             nc.sync.dma_start(wo_s_raw[32 * q : 32 * q + 8, :].bitcast(I32), wo_scales[:, 4 * q : 4 * q + 4, :].bitcast(I32))
-        v_w = keep.tile([P, S], U32, name="v_w", align_bytes=64)
-        for c in range(HALVES):
-            nc.vector.tensor_copy(
-                v_w[:, c * BANK : (c + 1) * BANK],
-                tab_w[:].bitcast(U32).indirect(offs_sb[:, c * BANK // 16 : (c + 1) * BANK // 16]),
-            )
-
-        wo_raw = keep.tile([P, GROUPS, N], I32, name="wo_raw", tag="tab_w", align_bytes=64)
+        wo_raw = keep.tile([P, GROUPS, N], I32, name="wo_raw", tag="picked_s", align_bytes=64)
         nc.sync.dma_start(wo_raw[:], wo_words.rearrange("a p c i -> p a (c i)").bitcast(I32))
 
         w_q = [keep.tile([P, H], U32, name="w_q%d" % i, align_bytes=64) for i in range(2)]
@@ -103,8 +108,11 @@ def tile_list_footage_pair_features_kernel(
         def round_weight(i, s):
             g, t = divmod(s, PACK)
             wb = ring.tile([P, 2, P, PACK], BF16, name="w_bf", tag="w_bf", bufs=3, align_bytes=64)
-            src = w_raw[(i, g)][:].rearrange("p j (m t) -> p m t j", t=PACK)[:, :, t : t + 2, :]
-            nc.scalar.copy(wb[:].rearrange("p t m j -> p m t j"), src)
+            pieces = w_raw[(i, g)]
+            width = P // len(pieces)
+            for n, raw in enumerate(pieces):
+                src = raw[:].rearrange("p j (m t) -> p m t j", t=PACK)[:, :, t : t + 2, :]
+                nc.scalar.copy(wb[:, :, n * width : (n + 1) * width, :].rearrange("p t m j -> p m t j"), src)
             rounded[(i, s)] = wb
 
         def quantise_weight(i, s):
@@ -210,8 +218,8 @@ def tile_list_footage_pair_features_kernel(
                 round_weight(0, ahead)
                 round_weight(1, ahead)
                 if ahead == PACK - 2:
-                    w_raw[(0, 1)] = load_weight(w1, 1, "w1_raw")
-                    w_raw[(1, 1)] = load_weight(w3, 1, "w3_raw")
+                    w_raw[(0, 1)] = load_weight(w1, 1, ["w1_raw_a", "w1_raw_b"])
+                    w_raw[(1, 1)] = load_weight(w3, 1, ["w3_raw"])
             pick_view(s)
             pick_second(s)
             first_max(s + 1, 0)
@@ -265,6 +273,7 @@ def tile_list_footage_pair_features_kernel(
         kept_half(last, 1)
 
         y_s = keep.tile([P, GROUPS, KEPT], U8, name="y_s", align_bytes=64)
+        y_q = [keep.tile([P, GROUPS, KEPT_HALF], I32, name="y_q%d" % c, align_bytes=64) for c in range(HALVES)]
         y_bf = {}
 
         def finish(g, c):
@@ -273,19 +282,20 @@ def tile_list_footage_pair_features_kernel(
             nc.vector.tensor_tensor(y[:], y_acc[(g, c)][:], a2[(g, c)], ALU.add)
             nc.sync.dma_start(out_0[g * GROUP : (g + 1) * GROUP, kept].rearrange("(p t) j -> p t j", t=PACK), y[:])
             y_bf[(g, c)] = keep.tile([P, KEPT_HALF, PACK], BF16, name="y_bf%d%d" % (g, c), align_bytes=64)
-            nc.scalar.copy(
+            cast = nc.vector.tensor_copy if (g, c) == (GROUPS - 1, HALVES - 1) else nc.scalar.copy
+            cast(
                 y_bf[(g, c)][:].rearrange("p (j i) t -> p j t i", i=4),
                 y[:].rearrange("p t (j i) -> p j t i", i=4),
             )
 
         def planes(g, c):
             kept = slice(c * KEPT_HALF, (c + 1) * KEPT_HALF)
-            y_q = keep.tile([P, KEPT_HALF], I32, name="y_q%d%d" % (g, c), align_bytes=64)
             nc.vector.quantize_mx(
-                out=y_q[:].bitcast(FP8X4), scales=y_s[:, g, kept],
+                out=y_q[c][:, g, :].bitcast(FP8X4), scales=y_s[:, g, kept],
                 in_=y_bf[(g, c)][:].rearrange("p j t -> p (j t)"),
             )
-            nc.sync.dma_start(out_1[g, :, kept, :].rearrange("p m t -> p (m t)").bitcast(I32), y_q[:])
+            if g == GROUPS - 1:
+                nc.sync.dma_start(out_1[:, :, kept, :].rearrange("g p m t -> p g (m t)").bitcast(I32), y_q[c][:])
 
         order = [(g, c) for c in range(HALVES) for g in range(GROUPS)]
         for n, (g, c) in enumerate(order):

from contextlib import ExitStack

import concourse.mybir as mybir

K, T, S, PAIRS, KEPT, H, N = 512, 4096, 1024, 512, 256, 1024, 1024
FLOPS = 2 * (3 * K * H * S + H * N * KEPT)

F32 = mybir.dt.float32
BF16 = mybir.dt.bfloat16
I32 = mybir.dt.int32
U32 = mybir.dt.uint32
U16 = mybir.dt.uint16
U8 = mybir.dt.uint8
FP8X4 = mybir.dt.float8_e4m3fn_x4
FP4X4 = mybir.dt.float4_e2m1fn_x4
ALU = mybir.AluOpType
ACT = mybir.ActivationFunctionType

P = 128
PACK = 4
GROUP = P * PACK
GROUPS = H // GROUP
SLICES = GROUPS * PACK
BANK = 512
HALVES = 2
KEPT_HALF = KEPT // HALVES
QUADS = 4
CLEAR_SPLIT = 2816


def tile_list_footage_pair_features_kernel(
    tc, tab_words, tab_scales, offs, pos1, pos2, pos3, pos4, w1, w2_words, w2_scales, w3, gain,
    wo_words, wo_scales, out_0, out_1, out_2,
):
    nc = tc.nc
    with ExitStack() as ctx:
        keep = ctx.enter_context(tc.tile_pool(name="keep", bufs=1))
        ring = ctx.enter_context(tc.tile_pool(name="ring", bufs=2))
        psum = ctx.enter_context(tc.psum_pool(name="psum", bufs=1))

        def load_list(src, name):
            lst = keep.tile(list(src.shape), U16, name=name)
            nc.sync.dma_start(lst[:], src)
            return lst

        def load_weight(w, g, tags):
            width = GROUP // len(tags)
            pieces = []
            for n, tag in enumerate(tags):
                raw = keep.tile([P, PACK, width], F32, name=tag, tag=tag, align_bytes=64)
                cols = slice(g * GROUP + n * width, g * GROUP + (n + 1) * width)
                nc.sync.dma_start(raw[:], w[:, cols].rearrange("(p j) c -> p j c", j=PACK))
                pieces.append(raw)
            return pieces

        def deal_columns(tag, raw, run):
            dealt = keep.tile(list(raw.shape), raw.dtype, name="dealt", tag=tag, align_bytes=64)
            nc.vector.tensor_copy(
                dealt[:].rearrange("p (g t m i) -> p g m t i", g=GROUPS, t=PACK, i=run),
                raw.rearrange("p (g m i t) -> p g m t i", g=GROUPS, t=PACK, i=run),
            )
            return dealt

        tab_s = keep.tile([P, T], U8, name="tab_s", tag="w3_raw", align_bytes=64)
        nc.vector.memset(tab_s[:, :CLEAR_SPLIT].bitcast(I32), 0)
        nc.gpsimd.memset(tab_s[:, CLEAR_SPLIT:].bitcast(I32), 0)
        w2_s_raw = keep.tile([P, H], U8, name="w2_s_raw", tag="scales_raw", align_bytes=64)
        nc.gpsimd.memset(w2_s_raw[:].bitcast(I32), 0)
        v_s = keep.tile([P, S], U8, name="v_s", align_bytes=64)
        nc.vector.memset(v_s[:].bitcast(I32), 0)
        offs_sb = load_list(offs, "offs_sb")
        w2_raw = keep.tile([P, H], U16, name="w2_raw", align_bytes=64)
        nc.sync.dma_start(w2_raw[:].bitcast(I32), w2_words[0].bitcast(I32))
        pos4_sb = load_list(pos4, "pos4_sb")
        pos2_sb = load_list(pos2, "pos2_sb")
        pos1_sb = load_list(pos1, "pos1_sb")
        pos3_sb = load_list(pos3, "pos3_sb")
        nc.sync.dma_start(tab_s[0:P:8, :].bitcast(I32), tab_scales[0].bitcast(I32))
        tab_w = keep.tile([P, T], I32, name="tab_w", tag="tab_w", align_bytes=64)
        nc.sync.dma_start(tab_w[:], tab_words[0].rearrange("p t i -> p (t i)").bitcast(I32))
        w_raw = {}
        w_raw[(0, 0)] = load_weight(w1, 0, ["w1_raw_a", "w1_raw_b"])
        gain_sb = keep.tile([P, GROUPS, PACK], F32, name="gain_sb")
        nc.sync.dma_start(gain_sb[:], gain.rearrange("(g p t) -> p g t", g=GROUPS, t=PACK))
        for q in range(QUADS):
            nc.gpsimd.dma_start(w2_s_raw[32 * q : 32 * q + 4, :].bitcast(I32), w2_scales[0, 4 * q : 4 * q + 4, :].bitcast(I32))

        w2_q = deal_columns("w2_q", w2_raw[:], 8)
        picked_s = keep.tile([P, S], U8, name="picked_s", tag="picked_s", align_bytes=64)
        nc.vector.tensor_copy(picked_s[:], tab_s[:].indirect(offs_sb[:]))
        for q in range(QUADS):
            nc.sync.dma_start(v_s[32 * q : 32 * q + 4, :].bitcast(I32), picked_s[32 * q : 32 * (q + 1) : 8, :].bitcast(I32))
        w_raw[(1, 0)] = load_weight(w3, 0, ["w3_raw"])
        v_w = keep.tile([P, S], U32, name="v_w", align_bytes=64)
        nc.vector.tensor_copy(v_w[:], tab_w[:].bitcast(U32).indirect(offs_sb[:]))
        w2_s = deal_columns("tab_w", w2_s_raw[:], 16)
        wo_s_raw = keep.tile([P, N], U8, name="wo_s_raw", tag="scales_raw", align_bytes=64)
        nc.gpsimd.memset(wo_s_raw[:].bitcast(I32), 0)
        for q in range(QUADS):
            nc.sync.dma_start(wo_s_raw[32 * q : 32 * q + 8, :].bitcast(I32), wo_scales[:, 4 * q : 4 * q + 4, :].bitcast(I32))
        wo_raw = keep.tile([P, GROUPS, N], I32, name="wo_raw", tag="picked_s", align_bytes=64)
        nc.sync.dma_start(wo_raw[:], wo_words.rearrange("a p c i -> p a (c i)").bitcast(I32))

        w_q = [keep.tile([P, H], U32, name="w_q%d" % i, align_bytes=64) for i in range(2)]
        w_qs = [keep.tile([P, H], U8, name="w_qs%d" % i, align_bytes=64) for i in range(2)]
        rounded = {}

        def round_weight(i, s):
            g, t = divmod(s, PACK)
            wb = ring.tile([P, 2, P, PACK], BF16, name="w_bf", tag="w_bf", bufs=3, align_bytes=64)
            pieces = w_raw[(i, g)]
            width = P // len(pieces)
            for n, raw in enumerate(pieces):
                src = raw[:].rearrange("p j (m t) -> p m t j", t=PACK)[:, :, t : t + 2, :]
                nc.scalar.copy(wb[:, :, n * width : (n + 1) * width, :].rearrange("p t m j -> p m t j"), src)
            rounded[(i, s)] = wb

        def quantise_weight(i, s):
            cols = slice(s * P, (s + 2) * P)
            nc.vector.quantize_mx(
                out=w_q[i][:, cols].bitcast(FP8X4),
                scales=w_qs[i][:, cols],
                in_=rounded[(i, s)][:].rearrange("p t m j -> p (t m j)"),
            )

        def product(tag, bufs, codes, scales, s, c):
            acc = psum.tile([P, BANK], F32, name="acc", tag=tag, bufs=bufs)
            cols = slice(s * P, (s + 1) * P)
            frames = slice(c * BANK, (c + 1) * BANK)
            nc.tensor.matmul_mx(
                out=acc[:], lhsT=codes(cols), lhsT_scale=scales[:, cols],
                rhs=v_w[:, frames].bitcast(FP8X4), rhs_scale=v_s[:, frames], start=True, stop=True,
            )
            return acc

        h12 = {}
        h = {}

        def first_max(s, c):
            acc1 = product("acc1", 2, lambda cols: w_q[0][:, cols].bitcast(FP8X4), w_qs[0], s, c)
            acc2 = product("acc2", 3, lambda cols: w2_q[:, cols].bitcast(FP4X4), w2_s, s, c)
            sum1 = ring.tile([P, BANK], F32, name="sum1", tag="sum1", bufs=4)
            nc.scalar.copy(sum1[:], acc1[:])
            h12[(s, c)] = ring.tile([P, BANK], F32, name="h12", tag="h12", bufs=8)
            nc.vector.tensor_tensor(h12[(s, c)][:], acc2[:], sum1[:], ALU.max)

        def second_max(s, c):
            acc3 = product("acc3", 3, lambda cols: w_q[1][:, cols].bitcast(FP8X4), w_qs[1], s, c)
            if c == 0:
                h[s] = ring.tile([P, S], F32, name="h", tag="h", bufs=2, align_bytes=64)
            nc.vector.tensor_tensor(h[s][:, c * BANK : (c + 1) * BANK], acc3[:], h12[(s, c)][:], ALU.max)

        a2_first = keep.tile([P, PACK, KEPT], F32, name="a2_first", align_bytes=64)
        a2 = {(0, c): a2_first[:, :, c * KEPT_HALF : (c + 1) * KEPT_HALF] for c in range(HALVES)}
        a2[(1, 0)] = keep.tile([P, PACK, KEPT_HALF], F32, name="a2_early", align_bytes=64)[:]
        x_bf = [keep.tile([P, KEPT, PACK], BF16, name="x_bf%d" % g, align_bytes=64) for g in range(GROUPS)]
        x_q = [keep.tile([P, KEPT], U32, name="x_q%d" % g, align_bytes=64) for g in range(GROUPS)]
        x_s = [keep.tile([P, KEPT], U8, name="x_s%d" % g, align_bytes=64) for g in range(GROUPS)]
        view = {}
        second = {}
        a1 = {}

        def pick_view(s):
            picked = ring.tile([P, KEPT], F32, name="picked4", tag="picked4")
            nc.vector.tensor_copy(picked[:], h[s][:].indirect(pos4_sb[:]))
            view[s] = ring.tile([P, KEPT], F32, name="view", tag="view", bufs=PACK + 1)
            nc.scalar.activation(view[s][:], picked[:], ACT.Tanh)

        def pick_second(s):
            second[s] = ring.tile([P, PAIRS], F32, name="second", tag="second", bufs=1, align_bytes=64)
            nc.vector.tensor_copy(second[s][:], h[s][:].indirect(pos2_sb[:]))

        def differences(s):
            a1[s] = ring.tile([P, PAIRS], F32, name="a1", tag="a1", bufs=PACK + 1, align_bytes=64)
            nc.vector.tensor_tensor(a1[s][:], h[s][:].indirect(pos1_sb[:]), second[s][:], ALU.subtract)

        def kept_pairs(s, dst, j0, j1):
            g, t = divmod(s, PACK)
            nc.vector.tensor_tensor(dst, a1[s][:].indirect(pos3_sb[:, j0 // 16 : j1 // 16]), view[s][:, j0:j1], ALU.mult)
            nc.scalar.activation(x_bf[g][:, j0:j1, t], dst, ACT.Copy, scale=gain_sb[:, g, t : t + 1])

        def kept_half(s, c):
            g, t = divmod(s, PACK)
            kept_pairs(s, a2[(g, c)][:, t, :], c * KEPT_HALF, (c + 1) * KEPT_HALF)

        def quantise_x(g, j0, j1):
            nc.vector.quantize_mx(
                out=x_q[g][:, j0:j1].bitcast(FP8X4), scales=x_s[g][:, j0:j1],
                in_=x_bf[g][:, j0:j1, :].rearrange("p j t -> p (j t)"),
            )

        wo_q = [keep.tile([P, N], I32, name="wo_q%d" % a, align_bytes=64) for a in range(GROUPS)]

        wo_s = keep.tile([P, N], U8, name="wo_s", align_bytes=64)
        for g in range(GROUPS):
            group = slice(g * GROUP, (g + 1) * GROUP)
            for t in range(0, PACK, 2):
                cols = slice(g * GROUP + t * P, g * GROUP + (t + 2) * P)
                moves = [(wo_q[a][:, cols], wo_raw[:, a, group]) for a in range(GROUPS)]
                moves.append((wo_s[:, cols], wo_s_raw[:, group]))
                for dst, src in moves:
                    nc.gpsimd.tensor_copy(
                        dst.rearrange("p (t m) -> p t m", t=2),
                        src.rearrange("p (m t) -> p t m", t=PACK)[:, t : t + 2, :],
                    )

        round_weight(0, 0)
        quantise_weight(0, 0)
        round_weight(1, 0)
        first_max(0, 0)
        first_max(0, 1)
        quantise_weight(1, 0)
        second_max(0, 0)
        second_max(0, 1)
        for s in range(SLICES - 1):
            ahead = s + 2
            if ahead % 2 == 0 and ahead < SLICES:
                round_weight(0, ahead)
                round_weight(1, ahead)
                if ahead == PACK - 2:
                    w_raw[(0, 1)] = load_weight(w1, 1, ["w1_raw_a", "w1_raw_b"])
                    w_raw[(1, 1)] = load_weight(w3, 1, ["w3_raw"])
            pick_view(s)
            pick_second(s)
            first_max(s + 1, 0)
            differences(s)
            first_max(s + 1, 1)
            if ahead % 2 == 0 and ahead < SLICES:
                quantise_weight(0, ahead)
                quantise_weight(1, ahead)
            if s == PACK:
                quantise_x(0, 0, KEPT)
            second_max(s + 1, 0)
            second_max(s + 1, 1)
            if s < PACK:
                kept_pairs(s, a2_first[:, s, :], 0, KEPT)
            else:
                kept_half(s, 0)

        y_acc = {}
        for c in range(HALVES):
            for g in range(GROUPS):
                tag, bufs = (("acc1", 2), ("acc2", 3))[c]
                y_acc[(g, c)] = psum.tile([P, PACK, KEPT_HALF], F32, name="y_acc", tag=tag, bufs=bufs)

        def y_passes(a, g, c):
            kept = slice(c * KEPT_HALF, (c + 1) * KEPT_HALF)
            for t in range(PACK):
                cols = slice(g * GROUP + t * P, g * GROUP + (t + 1) * P)
                nc.tensor.matmul_mx(
                    out=y_acc[(g, c)][:, t, :],
                    lhsT=wo_q[a][:, cols].bitcast(FP8X4), lhsT_scale=wo_s[4 * a :, cols],
                    rhs=x_q[a][:, kept].bitcast(FP8X4), rhs_scale=x_s[a][:, kept],
                    start=(a == 0 and t == 0), stop=(a == GROUPS - 1 and t == PACK - 1),
                )

        for c in range(HALVES):
            for g in range(GROUPS):
                y_passes(0, g, c)

        last = SLICES - 1
        pick_second(last)
        pick_view(last)
        differences(last)
        a2[(1, 1)] = ring.tile([P, PACK, KEPT_HALF], F32, name="a2_late", tag="second", bufs=1, align_bytes=64)[:]
        kept_half(PACK, 1)
        kept_half(last, 0)
        kept_half(PACK + 1, 1)
        kept_half(PACK + 2, 1)
        quantise_x(1, 0, KEPT_HALF)
        for g in range(GROUPS):
            y_passes(1, g, 0)
        kept_half(last, 1)

        y_s = keep.tile([P, GROUPS, KEPT], U8, name="y_s", align_bytes=64)
        y_q = [keep.tile([P, GROUPS, KEPT_HALF], I32, name="y_q%d" % c, align_bytes=64) for c in range(HALVES)]
        y_bf = {}

        def finish(g, c):
            kept = slice(c * KEPT_HALF, (c + 1) * KEPT_HALF)
            y = keep.tile([P, PACK, KEPT_HALF], F32, name="y%d%d" % (g, c), align_bytes=64)
            nc.vector.tensor_tensor(y[:], y_acc[(g, c)][:], a2[(g, c)], ALU.add)
            nc.sync.dma_start(out_0[g * GROUP : (g + 1) * GROUP, kept].rearrange("(p t) j -> p t j", t=PACK), y[:])
            y_bf[(g, c)] = keep.tile([P, KEPT_HALF, PACK], BF16, name="y_bf%d%d" % (g, c), align_bytes=64)
            cast = nc.vector.tensor_copy if (g, c) == (GROUPS - 1, HALVES - 1) else nc.scalar.copy
            cast(
                y_bf[(g, c)][:].rearrange("p (j i) t -> p j t i", i=4),
                y[:].rearrange("p t (j i) -> p j t i", i=4),
            )

        def planes(g, c):
            kept = slice(c * KEPT_HALF, (c + 1) * KEPT_HALF)
            nc.vector.quantize_mx(
                out=y_q[c][:, g, :].bitcast(FP8X4), scales=y_s[:, g, kept],
                in_=y_bf[(g, c)][:].rearrange("p j t -> p (j t)"),
            )
            if g == GROUPS - 1:
                nc.sync.dma_start(out_1[:, :, kept, :].rearrange("g p m t -> p g (m t)").bitcast(I32), y_q[c][:])

        order = [(g, c) for c in range(HALVES) for g in range(GROUPS)]
        for n, (g, c) in enumerate(order):
            finish(g, c)
            if n == 0:
                quantise_x(1, KEPT_HALF, KEPT)
                for late in range(GROUPS):
                    y_passes(1, late, 1)
            if n >= 2:
                planes(*order[n - 2])
        for g, c in order[-2:]:
            planes(g, c)
        for q in range(QUADS):
            queue = (nc.sync, nc.scalar)[q % 2]
            queue.dma_start(
                out_2[:, 4 * q : 4 * q + 4, :].rearrange("g r m -> r g m").bitcast(I32),
                y_s[32 * q : 32 * q + 4, :, :].bitcast(I32),
            )
